import numpy as np, ml_dtypes
CORES = [5,29,101,125,133,157,229,253]
N = 8
BF = ml_dtypes.bfloat16
def f(rng, *shape):
    return (rng.standard_normal(shape, dtype=np.float32) * np.exp2(rng.integers(-2, 3, shape[:-1] + (1,)))).astype(BF)
def wide(rng, *shape):
    v = f(rng, *shape).astype(np.float32); k = shape[:-2] + (1, shape[-1])
    return (v * np.exp2(rng.integers(-6, 7, k)) * (rng.random(k) > 0.0625)).astype(BF)
def gentries(a):
    return np.ascontiguousarray(a.reshape(8, 16, -1).transpose(0, 2, 1)).reshape(8, -1)
def gtable(e):
    e = np.asarray(e); return np.ascontiguousarray(e.reshape(8, -1, 16).transpose(0, 2, 1)).reshape(128, -1).astype(np.int32)
H, C, M, W = 3072, 2048, 3, 384
JM = 2.0 ** -12
def positive(v):
    return np.abs(v.astype(np.float32)).astype(BF)
def glists(e):
    return np.stack([gtable(v) for v in e])
def lastplaces(rng):
    c = np.sort(np.argsort(rng.random((N, 8, H - 1)), -1)[..., :C - 1], -1)
    return np.concatenate([c, np.full((N, 8, 1), H - 1)], -1)
def classes(e):
    return np.stack([np.stack([np.searchsorted(v, np.arange(H)) for v in u]) for u in e])
def setup_inputs(rng):
    e = lastplaces(rng)
    return {"w": positive(f(rng, N, 128, W)), "pm": glists(np.argsort(rng.random((N, 8, H)), -1)), "cl": glists(classes(e)), "en": glists(e),
            "al": rng.integers(0, 2 ** M, (N, 8, C)).astype(np.int32), "tg": rng.integers(0, 2, (N, 128, M)).astype(np.int32),
            "st": (0.5 + 0.5 * rng.random((N, 128, M))).astype(np.float32), "ju": (JM * rng.random((N, 128, M))).astype(np.float32), "mi": (0.25 + 0.75 * rng.random((N, 128, M))).astype(np.float32)}
def setup_inputs_runs(rng):
    d = setup_inputs(rng); b = rng.integers(0, C, (N, 8, 1)); b[:, 0] = 0; b[:, 1] = C - 1
    c = np.arange(C).reshape(1, 1, C); e = c + (H - C) * (c >= b); d["cl"] = glists(classes(e)); d["en"] = glists(e)
    p = np.argsort(rng.random((N, 8, H)), -1); p[:, 2] = np.arange(H); p[:, 3] = np.arange(H)[::-1]; d["pm"] = glists(p); return d
def setup_inputs_still(rng):
    d = setup_inputs(rng); m = rng.random((N, 1, M)) < 0.5; m[:, :, 0] = True
    d["st"] = np.where(m, np.float32(1), d["st"]); d["ju"] = np.where(m, np.float32(0), d["ju"])
    d["mi"] = np.where(rng.random((N, 128, M)) < 0.25, np.float32(1), d["mi"]); return d
def setup_inputs_sharp(rng):
    d = setup_inputs(rng); d["mi"] = np.full((N, 128, M), 0.25, np.float32)
    d["ju"] = np.where(rng.random((N, 128, M)) < 0.5, np.float32(JM), d["ju"]); d["st"] = np.where(rng.random((N, 128, M)) < 0.25, np.float32(0.5), d["st"])
    q = rng.integers(0, N); v = int(rng.integers(0, 2 ** M)); d["al"][q, 0] = v; z = (v >> np.arange(M)) & 1
    d["tg"][q, 0] = 1 - z; d["tg"][q, 1] = z; return d
def setup_inputs_few(rng):
    d = setup_inputs(rng); h = rng.integers(0, H, 128); h[0] = 0; h[127] = H - 1
    v = np.zeros((128, H), np.float32); v[np.arange(128), h] = 1 + 7 * rng.random(128)
    d["w"] = np.ascontiguousarray(v.reshape(128, N, W).transpose(1, 0, 2)).astype(BF); return d
def setup_inputs_spread(rng):
    d = setup_inputs(rng); d["w"] = positive(wide(rng, N, 128, W)); b = rng.random((N, 8, C, M)) < rng.random((N, 8, 1, M))
    d["al"] = np.sum(b * (1 << np.arange(M)), -1).astype(np.int32); return d
def check_inputs(d):
    bad = []; w = d["w"].astype(np.float64)
    if not np.isfinite(w).all() or (w < 0).any() or (w > 2.0 ** 20).any() or (np.sum(w, (0, 2)) < 1).any(): bad.append("w")
    p, c, e = [np.stack([gentries(a) for a in d[k]]) for k in ("pm", "cl", "en")]
    if (np.sort(p, -1) != np.arange(H)).any(): bad.append("pm")
    if (e < 0).any() or (e[..., -1] != H - 1).any() or (e[..., 1:] <= e[..., :-1]).any(): bad.append("en")
    if (c != classes(e)).any(): bad.append("cl")
    if (d["al"] < 0).any() or (d["al"] >= 2 ** M).any(): bad.append("al")
    if (d["tg"] < 0).any() or (d["tg"] > 1).any(): bad.append("tg")
    for k, lo, hi in (("st", 0.5, 1.0), ("ju", 0.0, JM), ("mi", 0.25, 1.0)):
        if not ((d[k] >= lo) & (d[k] <= hi)).all(): bad.append(k)
    return bad
def reference(w, pm, cl, en, al, tg, st, ju, mi):
    x = w.astype(np.float64).transpose(1, 0, 2).reshape(128, H); y = np.zeros((N, 128, H), np.float64)
    for r in range(N):
        x = np.take_along_axis(x, np.repeat(gentries(pm[r]), 16, 0), 1)
        a = np.repeat(np.take_along_axis(al[r], gentries(cl[r]), 1), 16, 0)
        for s in range(M):
            stay, jump, miss = [v[r][:, s:s + 1].astype(np.float64) for v in (st, ju, mi)]
            e = np.where(((a >> s) & 1) == tg[r][:, s:s + 1], 1.0, miss)
            x = e * (stay * x + jump * np.sum(x, 1, keepdims=True))
        y[r] = x
    return {"y": y.astype(np.float32)}

@@ -1,0 +1,469 @@
+from concourse.bass import DstId, RemoteDMATransfer
+from concourse.mybir import AluOpType, AxisListType, ActivationFunctionType
+
+N, H, CH, NL = 8, 3072, 384, 24
+SIM_CORES = 256
+F, B, I, U = "float32", "bfloat16", "int32", "uint16"
+
+SCRATCH = {}
+for _d, _bufs in (
+        (I, dict(alt=128, cli=192, pmi=192, pa=192, pb=192, tgi=4, gi=128)),
+        (U, dict(clu=192, offa=192, codea=192, offb=96, codeb=96)),
+        (B, dict(altb=128, alw=2048, arow=H, oneb=144, zin=144, iext=144, zb=144, repb=1024, lw=CH)),
+        (F, dict(pmf=192, par=12, val=192, oh=768, junk=2 * CH, n4=4, sm=160, zall=144, rep=1024, turn=128, bd=128,
+                 gm=128, bits=24, seg=12, lv=192, lt=384, tabs=384, win=H, win2=H, rr=4 * CH, tf=192, t1=CH, t2=CH,
+                 z1=CH, z2=CH, zz=2 * CH, xm=CH, ys=H, uc=32, pp=192, bt=64))):
+    for _n, _c in _bufs.items():
+        SCRATCH[_n] = ("sbuf", [128, _c], _d)
+for _n, _c, _d in (("sw", 48, B), ("dw", 48, B), ("sv", NL, F), ("dv", NL, F), ("dy", CH, F)):
+    SCRATCH[_n] = ("dram", [N, 128, _c], _d)
+for _k in range(8):
+    SCRATCH["ps%d" % _k] = ("psum", [128, 512], F)
+SEMAPHORES = ["cv", "cs", "cp", "cg", "ls", "aw", "avs", "avd", "at", "ay", "az"] + ["d%d" % _k for _k in range(24)]
+WIDTH = {"lv": NL, "lt": 48, "ys": CH}
+
+
+def bits_of(engines):
+    m = 0
+    for e in engines:
+        m |= 1 << e
+    return m
+
+
+def deal(engines, sizes):
+    out, k = [], 0
+    for s in sizes:
+        out.append(bits_of(engines[k:k + s])); k += s
+    return out
+
+
+def make_routes(cores, topo):
+    cross = [[d for d in range(N) if d != r and not topo.may_write(cores[r], cores[d])] for r in range(N)]
+    same = [[d for d in range(N) if d != r and topo.may_write(cores[r], cores[d])] for r in range(N)]
+    near = [[c for c in topo.cores_of(cores[r]) if topo.die(c) != topo.die(cores[r]) and topo.may_write(c, cores[cross[r][0]])]
+            for r in range(N)]
+    far = [[c for c in range(SIM_CORES) if topo.mates(c, cores[d]) and topo.die(c) == topo.die(cores[d])
+            and topo.may_write(c, cores[d])][0] for d in range(N)]
+    calls, steps, arrive = {}, {}, {}
+    far_w, far_y = [[] for _ in range(N)], [[] for _ in range(N)]
+    for r in range(N):
+        me = cores[r]
+        off = topo.engines(me, cores[same[r][0]])
+        on = [e for e in topo.engines(me, near[r][0]) if e not in off]
+        by = sorted(cross[r], key=lambda d: (cross[r].index(d) - cross[d].index(r)) % len(cross[r]))
+        a0, a1 = near[r][0], near[r][1]
+        via = {by[0]: a0, by[1]: a1, by[2]: a0, by[3]: a1}
+        c = {}
+        m, n = deal(off, [2, 2, 2, 1, 1]), deal(on, [4, 4])
+        c["w"] = [[(far[by[2 + k]], m[k], ("sw", by[2 + k]), ("dw", r), "aw") for k in range(2)]
+                  + [(cores[d], m[2 + k], ("sw", d), ("dw", r), "aw") for k, d in enumerate(same[r])]
+                  + [(via[by[k]], n[k], ("sw", by[k]), ("dw", by[k]), "aw") for k in range(2)]]
+        m = deal(off, [2, 2, 2])
+        c["t"] = [[(a, n[k], ("lt", r), ("lt", r), "at") for k, a in enumerate((a0, a1))]
+                  + [(cores[d], m[k], ("lt", r), ("lt", r), "at") for k, d in enumerate(same[r])]]
+        n = deal(on, [2, 2, 2, 2])
+        hand = [(via[d], n[k], ("sv", d), ("dv", d), "avd") for k, d in enumerate(by)]
+        tiles = [(cores[d], m[k], ("sv", d), ("lv", r), "avs") for k, d in enumerate(same[r])]
+        rows = [(cores[d], m[k], ("sv", d), ("dv", r // 2), "avd") for k, d in enumerate(same[r])]
+        c["v"] = [hand + rows, tiles] if r % 2 == 0 else [hand + tiles]
+        for d in same[r]:
+            c["y%d" % d] = [[(cores[d], bits_of(off), ("ys", d), ("dy", r), "ay")]]
+        for k in range(2):
+            c["y%d" % by[k]] = [[(via[by[k]], bits_of(on), ("ys", by[k]), ("dy", by[k]), "ay")]]
+            d = by[2 + k]
+            c["y%d" % d] = [[(far[d], bits_of(off), ("ys", d), ("dy", r), ("ay", "az")[k])]]
+            far_w[d].append(r); far_y[d].append((("ay", "az")[k], r))
+        calls[me] = c
+        for k, a in enumerate((a0, a1)):
+            e = topo.engines(a, cores[by[0]]); mine = [by[k], by[2 + k]]
+            if r % 2 == 0:
+                m = deal(e, [2, 2, 2, 2])
+                fv = [(cores[d], m[j], ("dv", d), ("dv", r // 2), "avd") for j, d in enumerate(mine)] \
+                    + [(cores[d], m[2 + j], ("dv", d), ("lv", r), "avs") for j, d in enumerate(mine)]
+            else:
+                m = deal(e, [4, 4])
+                fv = [(cores[d], m[j], ("dv", d), ("lv", r), "avs") for j, d in enumerate(mine)]
+            m = deal(e, [4, 4])
+            steps[a] = [("aw", [(cores[by[k]], bits_of(e), ("dw", by[k]), ("dw", r), "aw")]),
+                        ("avd", fv),
+                        ("at", [(cores[d], m[j], ("lt", r), ("lt", r), "at") for j, d in enumerate(mine)]),
+                        ("ay", [(cores[by[k]], bits_of(e), ("dy", by[k]), ("dy", r), "ay")])]
+    for d in range(N):
+        e = topo.engines(far[d], cores[d]); m = deal(e, [4, 4])
+        steps[far[d]] = [("aw", [(cores[d], m[j], ("dw", r), ("dw", r), "aw") for j, r in enumerate(far_w[d])])] \
+            + [(s, [(cores[d], bits_of(e), ("dy", r), ("dy", r), "ay")]) for s, r in sorted(far_y[d])]
+    every = [call for c in calls.values() for ph in c.values() for call in ph] + [call for s in steps.values() for _, call in s]
+    for call in every:
+        for dst, mask, _, _, sem in call:
+            arrive[(dst, sem)] = arrive.get((dst, sem), 0) + bin(mask).count("1")
+    return calls, steps, arrive
+
+
+def remote_call(g, core, T, topo, call):
+    def side(key):
+        name, k = key
+        return T[name][:, WIDTH[name] * k:WIDTH[name] * (k + 1)] if name in WIDTH else T[name][k]
+    if len(call) == 1:
+        dst, mask, a, b, sem = call[0]
+        rid, pid = topo.addr(dst, core)
+        g.remote_dma(side(b), side(a), T.sem[sem], T.sem.ls, pid, rid, mask)
+    else:
+        tr = []
+        for dst, mask, a, b, sem in call:
+            rid, pid = topo.addr(dst, core)
+            tr.append(RemoteDMATransfer(dst_ids=[DstId(rid=rid, pnc=pid)], dma_engine_mask=mask, remote_sem=T.sem[sem],
+                                        src=side(a), dst=side(b)))
+        g.remote_dma_fused(tr, local_sem=T.sem.ls)
+    return sum(bin(t[1]).count("1") for t in call)
+
+
+def emit(g, T, ops):
+    queue = {"v": g.vector, "s": g.scalar, "p": g.tensor, "g": g, "y": g.sync}
+    deps, needed = [], set()
+    for n, (q, call, rd, wr, done) in enumerate(ops):
+        mine = set()
+        for k in range(n):
+            q2, call2, rd2, wr2, done2 = ops[k]
+            hit = False
+            for (na, lo, hi) in rd:
+                bank = na.startswith("ps") and q2 != q
+                for (nb, l2, h2) in wr2 + (rd2 if bank else []):
+                    if na == nb and (bank or (lo < h2 and l2 < hi)):
+                        hit = True
+            if not (q2 == q and ("+", 0, 0) in rd) and not (isinstance(done, str) and done == done2):
+                for (na, lo, hi) in wr:
+                    bank = na.startswith("ps") and q2 != q
+                    for (nb, l2, h2) in wr2 + rd2:
+                        if na == nb and (bank or (lo < h2 and l2 < hi)):
+                            hit = True
+            if hit and call is not None:
+                mine.add(k)
+        last = {}
+        for k in mine:
+            key = ops[k][0] if ops[k][4] is None else ("x", k)
+            last[key] = max(last.get(key, -1), k)
+        deps.append(sorted(last.values(), reverse=True)); needed.update(last.values())
+    groups, total = {}, {}
+    for q, call, rd, wr, done in ops:
+        if isinstance(done, str) and done != "remote":
+            groups.setdefault(done, "d%d" % len(groups))
+            total[groups[done]] = total.get(groups[done], 0) + 16
+        elif isinstance(done, tuple):
+            total[done[0]] = done[1]
+    mark, clock, known, count = {}, {}, {q: {} for q in queue}, {}
+    for n, (q, call, rd, wr, done) in enumerate(ops):
+        for k in deps[n]:
+            sem, v = mark[k]
+            if known[q].get(sem, 0) < v:
+                queue[q].wait_ge(T.sem[sem], v)
+                known[q][sem] = v
+                for s2, v2 in clock[k].items():
+                    known[q][s2] = max(known[q].get(s2, 0), v2)
+        clock[n] = dict(known[q]) if call is not None else {}
+        if call is None:
+            mark[n] = done
+        elif done == "remote":
+            total["ls"] = total.get("ls", 0) + call()
+        elif done is None:
+            ins = call()
+            if n in needed:
+                sem = "c" + q
+                count[sem] = count.get(sem, 0) + 1
+                ins.then_inc(T.sem[sem], 1)
+                mark[n] = (sem, count[sem]); total[sem] = count[sem]
+        else:
+            call().then_inc(T.sem[groups[done]], 16)
+            mark[n] = (groups[done], total[groups[done]]); clock[n] = {}
+    for sem, v in total.items():
+        if all(known[q].get(sem, 0) < v for q in queue):
+            g.wait_ge(T.sem[sem], v)
+
+
+def rank_program(g, core, T, topo):
+    cores = list(T.cores)
+    calls, steps, arrive = make_routes(cores, topo)
+    rank = T.rank_of(core)
+    if rank is None:
+        sent = 0
+        for sem, call in steps.get(core, []):
+            g.wait_ge(T.sem[sem], arrive[(core, sem)])
+            sent += remote_call(g, core, T, topo, call)
+        if sent:
+            g.wait_ge(T.sem.ls, sent)
+        return
+    A, ACT = AluOpType, ActivationFunctionType
+    ops = []
+
+    def R(name, lo=0, hi=None, step=1):
+        hi = SCRATCH[name][1][1] if hi is None else hi
+        return (T[name][:, lo:hi:step] if step > 1 else T[name][:, lo:hi], [(name, lo, hi)])
+
+    def S(name, k, n):
+        return R(name, n * k, n * k + n)
+
+    def ind(win, off):
+        return (win[0].indirect(off[0]), win[1] + off[1])
+
+    def reg(*xs):
+        return [t for x in xs if isinstance(x, tuple) for t in x[1]]
+
+    def ap(x):
+        return x[0] if isinstance(x, tuple) else x
+
+    def copy(o, i):
+        ops.append(("v", lambda: g.vector.tensor_copy(o[0], i[0]), reg(i), reg(o), None))
+
+    def tt(o, a, b, op):
+        ops.append(("v", lambda: g.vector.tensor_tensor(o[0], a[0], b[0], op), reg(a, b), reg(o), None))
+
+    def ts(o, a, s1, op0, s2=None, op1=None):
+        if s2 is None:
+            ops.append(("v", lambda: g.vector.tensor_scalar(o[0], a[0], ap(s1), None, op0), reg(a, s1), reg(o), None))
+        else:
+            ops.append(("v", lambda: g.vector.tensor_scalar(o[0], a[0], ap(s1), ap(s2), op0, op1), reg(a, s1, s2), reg(o), None))
+
+    def memset(o, c):
+        ops.append(("v", lambda: g.vector.memset(o[0], c), [], reg(o), None))
+
+    def act(o, i, scale=None, acc=None):
+        if acc is not None:
+            ops.append(("s", lambda: g.scalar.activation(o[0], i[0], ACT.Copy, accum_out=acc[0]), reg(i), reg(o, acc), None))
+        elif scale is not None:
+            ops.append(("s", lambda: g.scalar.activation(o[0], i[0], ACT.Copy, scale=scale[0]), reg(i, scale), reg(o), None))
+        else:
+            ops.append(("s", lambda: g.scalar.activation(o[0], i[0], ACT.Copy), reg(i), reg(o), None))
+
+    def mm(o, l, r, start=True, stop=True):
+        ops.append(("p", lambda: g.tensor.matmul(o[0], l[0], r[0], start, stop),
+                    reg(l, r) + ([] if start else [("+", 0, 0)]), reg(o), None))
+
+    def select(o, i, pattern, op, base, cm):
+        ops.append(("g", lambda: g.affine_select(o[0], i[0], pattern, op, 0.0, base, cm), reg(i), reg(o), None))
+
+    def iota(o, pattern, base, cm, small):
+        if small:
+            ops.append(("g", lambda: g.iota(o[0], pattern, base, cm, allow_small_or_imprecise_dtypes=True), [], reg(o), None))
+        else:
+            ops.append(("g", lambda: g.iota(o[0], pattern, base, cm), [], reg(o), None))
+
+    def dma(q, o, i, group):
+        e = g.sync if q == "y" else g.scalar
+        ops.append((q, lambda: e.dma_start(o[0], i[0]), reg(i), reg(o), group))
+
+    def send(phase, *reads):
+        for call in calls[core][phase]:
+            ops.append(("g", lambda call=call: remote_call(g, core, T, topo, call), reg(*reads), [], "remote"))
+
+    def landed(sem, name, slots, width=1):
+        ops.append(("g", None, [], [(name, width * k, width * k + width) for k in slots], (sem, arrive[(core, sem)])))
+
+    def D(name, lo, hi=None):
+        return (T[name][lo], [(name, lo, lo + 1)]) if hi is None else (T[name][lo:hi], [(name, lo, hi)])
+
+    def ext(x):
+        return (x, [])
+
+    q0 = 16 * rank
+    others = [r for r in range(N) if r != rank]
+    landed("aw", "dw", others)
+    landed("avs", "lv", others, NL)
+    landed("avd", "dv", [u for u in range(4) if 2 * u != rank])
+    landed("at", "lt", others, 48)
+    landed("ay", "dy", others)
+
+    dma("y", R("alt"), ext(T.al[:]), "al")
+    dma("s", R("cli"), ext(T.cl[:]), "cl")
+    dma("y", D("sw", 0, N), ext(T.w[:]), "sw")
+    dma("s", R("tgi", 0, 3), ext(T.tg[:]), "par")
+    dma("s", R("par", 8, 11), ext(T.mi[:]), "par")
+    dma("y", R("pmi"), ext(T.pm[:]), "pm")
+    dma("s", R("par", 0, 3), ext(T.st[:]), "par")
+    dma("s", R("par", 4, 7), ext(T.ju[:]), "par")
+    dma("y", D("dw", rank), ext(T.w[q0:q0 + 16, :]), "ow")
+    st = [R("par", s, s + 1) for s in range(3)]
+    ju = [R("par", 4 + s, 5 + s) for s in range(3)]
+    mi = [R("par", 8 + s, 9 + s) for s in range(3)]
+
+    memset(R("oneb"), 1.0)
+    memset(R("zin"), 1.0 / 32)
+    memset(R("win2", 0, 2048), 1.0)
+    select(R("iext"), R("oneb"), [[-1, 144]], A.is_equal, 0, 1)
+    iota(S("bits", 0, 8), [[0, 4], [1, 2]], 0, 0, True)
+    iota(S("bits", 1, 8), [[0, 2], [1, 2], [0, 2]], 0, 0, True)
+    iota(S("bits", 2, 8), [[1, 2], [0, 4]], 0, 0, True)
+    select(R("zb"), R("zin"), [[-16, 9], [256, 16]], A.is_equal, -3840, 1)
+    send("w", D("sw", 0, N))
+    select(R("rep"), R("win2", 0, 1024), [[-16, 8], [0, 8], [-1, 16]], A.is_equal, 0, 1)
+    select(R("bd"), R("win2", 0, 128), [[-16, 8], [0, 16]], A.is_ge, 0, 1)
+    iota(R("seg"), [[0, 3], [1, 4]], 0, 0, True)
+    iota(R("gi"), [[0, 8], [-1, 16]], 16, 1, False)
+    select(R("zall"), R("win2", 0, 144), [[-16, 9], [256, 16]], A.is_ge, -3840, 1)
+    select(R("bd"), R("bd"), [[16, 8], [0, 16]], A.is_ge, 15, -1)
+    select(R("turn"), R("win2", 0, 128), [[-1, 8], [-8, 16]], A.is_equal, 0, 1)
+    select(R("zall"), R("zall"), [[16, 9], [0, 16]], A.is_ge, 15, -1)
+
+    copy(R("altb"), R("alt"))
+    for e in range(16):
+        mm(S("ps%d" % (e // 4), e % 4, 128), R("iext", e, e + 128), R("altb"))
+    copy(R("clu"), R("cli"))
+    E = [S("sm", s, 8) for s in range(3)]
+    E01, E12, E012, b0, b1, x0, x1 = [S("sm", 3 + k, 8) for k in range(7)]
+    W1, W2, AA, K0, K1, K2 = [S("lt", 6 * rank + k, 8) for k in range(6)]
+    copy(R("sm", 80, 83), R("tgi", 0, 3))
+    for s in range(3):
+        ts(E[s], S("bits", s, 8), R("sm", 80 + s, 81 + s), A.is_equal, mi[s], A.max)
+    copy(S("alw", 0, 512), R("ps0"))
+    act(S("alw", 2, 512), R("ps2"))
+    copy(S("alw", 1, 512), R("ps1"))
+    act(S("alw", 3, 512), R("ps3"))
+    copy(R("arow", 0, 1536), ind(R("alw"), R("clu", 0, 96)))
+    act(R("arow", 1536, H), ind(R("alw"), R("clu", 96, 192)))
+    for k in range(16):
+        mm(R("ps4", 0, 192), R("zb", 15 - k, 143 - k), R("arow", k, H, 16), k == 0, k == 15)
+    act(R("repb"), R("rep"))
+    if rank % 2:
+        ts(R("pa"), R("pmi"), 15, A.bitwise_and)
+        ts(R("pb"), R("pmi"), 4, A.arith_shift_right)
+    tt(E01, E[0], E[1], A.mult)
+    tt(E12, E[1], E[2], A.mult)
+    ts(W1, E[0], st[0], A.mult)
+    ts(K2, E[2], ju[2], A.mult)
+    if rank % 2:
+        ts(R("tf"), R("pa"), 192.0, A.mult)
+    ts(R("sm", 96, 100), R("sm", 0, 4), ju[0], A.mult)
+    ts(R("sm", 104, 108), R("sm", 8, 12), ju[1], A.mult)
+    tt(E012, E01, E[2], A.mult)
+    if rank % 2:
+        tt(R("pmf"), R("tf"), R("pb"), A.add)
+    else:
+        copy(R("pmf"), R("pmi"))
+    ts(W2, E01, st[0], A.mult, st[1], A.mult)
+    ts(b1, E12, st[2], A.mult, ju[1], A.mult)
+    ts(R("sm", 100, 104), R("sm", 24, 28), st[1], A.mult, ju[0], A.mult)
+    ts(x0, E012, st[1], A.mult, st[2], A.mult)
+    ts(R("seg"), R("seg"), 1.0, A.min)
+    ts(AA, x0, st[0], A.mult)
+    ts(b0, x0, ju[0], A.mult)
+    tt(R("val"), R("pmf"), R("ps4", 0, 192), A.add)
+    dma("y", D("sv", 0, N), R("val"), "sv")
+    own = (T.val[q0:q0 + 16, :], [("val", 0, 192)])
+    dma("y", S("lv", rank, NL), own, "olv")
+    if rank % 2 == 0:
+        dma("y", D("dv", rank // 2), own, "odv")
+    send("v", D("sv", 0, N))
+
+    ts(R("pa"), R("ps4", 0, 192), 32.0, A.mult)
+    ts(R("pb"), R("pa"), 3, A.bitwise_and)
+    for k in range(4):
+        ts(S("oh", k, 192), R("pb"), float(k), A.is_equal)
+        act(S("oh", k, 192), S("oh", k, 192), acc=S("n4", k, 1))
+    ts(R("gi"), R("gi"), 15, A.bitwise_and)
+    for k in range(3):
+        mm(S("ps5", k, 4), R("bd"), R("n4"))
+    ts(R("gm"), R("gi"), 0.0, A.is_equal)
+    tt(R("sm", 112, 124), R("sm", 96, 108), R("ps5", 0, 12), A.mult)
+    ops.append(("v", lambda: g.vector.tensor_tensor_scan(T.sm[:, 128:140], T.seg[:], T.sm[:, 112:124], 0.0, A.mult, A.add),
+                reg(R("seg"), R("sm", 112, 124)), reg(R("sm", 128, 140)), None))
+    m10, m20, m21 = R("sm", 131, 132), R("sm", 135, 136), R("sm", 139, 140)
+    x2, x3 = R("sm", 144, 152), R("sm", 152, 160)
+    ts(x0, K2, m21, A.mult)
+    ts(x1, K2, m20, A.mult)
+    tt(K1, x0, b1, A.add)
+    tt(x2, x1, b0, A.add)
+    ts(x3, K1, m10, A.mult)
+    tt(K0, x2, x3, A.add)
+    send("t", S("lt", rank, 48))
+    memset(R("win2", 2048, H), 1.0)
+
+    def replicate(src, sel):
+        for c in range(8):
+            bank = R("ps%d" % (c % 4), 0, CH)
+            mm(bank, S(sel, c, 128), src)
+            act(S("win", c, CH), bank)
+
+    dma("s", R("lw"), D("dw", 0, N), "lw")
+    replicate(R("lw"), "repb")
+
+    def unpack(bank, lo, hi, off, code):
+        copy(R(off, lo, hi), R(bank, lo, hi))
+        copy(R("tf", lo, hi), R(off, lo, hi))
+        tt(R("pmf", lo, hi), R(bank, lo, hi), R("tf", lo, hi), A.subtract)
+        ts(R(code, lo, hi), R("pmf", lo, hi), 32.0, A.mult)
+
+    def compose(u):
+        src = ind(R("win2"), S("offa", 2 * u + 1, NL))
+        if u == 0:
+            ts(S("rr", u, CH), src, S("gm", u, 1), A.mult)
+        else:
+            act(S("rr", u, CH), src, scale=S("gm", u, 1))
+
+    def fold(u0, u1):
+        for k in range(16):
+            mm(R("ps5", NL * u0, NL * u1), R("zall", 15 - k, 143 - k), R("rr", CH * u0 + k, CH * u1, 16), k == 0, k == 15)
+
+    for c in range(8):
+        dma("ys"[c % 2], (T.win2[16 * c:16 * c + 4, :], [("win2", 0, H)]), D("dv", 0, 4), "w2")
+    mm(R("ps4", 0, 192), R("turn"), R("lv"))
+    unpack("ps4", 0, 192, "offa", "codea")
+    mm(R("ps6", 0, 384), S("rep", rank, 128), R("lt"))
+    act(R("tabs"), R("ps6", 0, 384))
+    compose(0)
+    fold(0, 1)
+    for u in range(1, 4):
+        compose(u)
+
+    def tb(r, k):
+        return S("tabs", 6 * r + k, 8)
+
+    def block(r, x, code, x2nd, code2nd, out):
+        u = [S("uc", 4 * r + k, 1) for k in range(3)]
+        p = [S("pp", 3 * r + k, 8) for k in range(3)]
+        bank = R(("ps7", "ps4")[r % 2], 0, 8)
+        bt = S("bt", r, 8)
+        tt(R("z1"), ind(tb(r, 0), code), x, A.mult)
+        act(S("junk", 0, CH), x, acc=u[0])
+        act(p[0], tb(r, 3), scale=u[0])
+        mm(bank, R("gm"), p[0], True, False)
+        tt(R("z2"), ind(tb(r, 1), code), x, A.mult)
+        act(S("junk", 1, CH), R("z1"), acc=u[1])
+        act(p[1], tb(r, 4), scale=u[1])
+        mm(bank, R("gm"), p[1], False, False)
+        if r == 0:
+            unpack("ps5", 0, NL, "offb", "codeb")
+            act(R("t2"), ind(R("win"), S("offb", 0, NL)))
+        ops.append(("v", lambda: g.vector.tensor_reduce(u[2][0], T.z2[:], AxisListType.X, A.add), reg(R("z2")), reg(u[2]), None))
+        ts(p[2], tb(r, 5), u[2], A.mult)
+        mm(bank, R("gm"), p[2], False, True)
+        if r == 0:
+            fold(1, 4)
+        tt(S("zz", r % 2, CH), ind(tb(r, 2), code2nd), x2nd, A.mult)
+        copy(bt, bank)
+        tt(out, ind(bt, code2nd), S("zz", r % 2, CH), A.add)
+
+    def ship(r):
+        if r == rank:
+            dma("y", D("dy", rank), S("ys", r, CH), "oy")
+        else:
+            send("y%d" % r, S("ys", r, CH))
+
+    for u in range(4):
+        r = 2 * u
+        ca, cb = S("codea", r, NL), S("codea", r + 1, NL)
+        copy(R("t1"), ind(R("win"), S("offa", r, NL)))
+        if u:
+            act(R("t2"), ind(R("win"), S("offb", u, NL)))
+        block(r, R("t1"), ca, R("t2"), S("codeb", u, NL), R("xm"))
+        block(r + 1, R("xm"), cb, R("xm"), cb, S("ys", r + 1, CH))
+        ship(r + 1)
+        if u < 3:
+            replicate(S("ys", r + 1, CH), "rep")
+        tt(S("zz", 0, CH), ind(tb(r, 2), ca), R("t1"), A.mult)
+        tt(S("ys", r, CH), ind(S("bt", r, 8), ca), S("zz", 0, CH), A.add)
+        ship(r)
+        if u == 0:
+            unpack("ps5", NL, 4 * NL, "offb", "codeb")
+
+    for c in range(8):
+        q = "s" if rank >= N - 2 and c % 2 else "y"
+        dma(q, ext(T.y[:, CH * c:CH * c + CH]), (T.dy[:, 16 * c:16 * c + 16, :], [("dy", 0, N)]), "out")
+    emit(g, T, ops)

@@ -1,26 +1,31 @@
 from concourse.bass import DstId, RemoteDMATransfer
-from concourse.mybir import AluOpType, AxisListType, ActivationFunctionType
+from concourse.mybir import AluOpType, ActivationFunctionType
 
 N, H, CH, NL = 8, 3072, 384, 24
 SIM_CORES = 256
+LATE = 6
+FIRST = (0, 3, 6)
+ROWS = (0, 1, 3, 4, 6)
 F, B, I, U = "float32", "bfloat16", "int32", "uint16"
 
 SCRATCH = {}
 for _d, _bufs in (
-        (I, dict(alt=128, cli=192, pmi=192, pa=192, pb=192, tgi=4, gi=128)),
-        (U, dict(clu=192, offa=192, codea=192, offb=96, codeb=96)),
-        (B, dict(altb=128, alw=2048, arow=H, oneb=144, zin=144, iext=144, zb=144, repb=1024, lw=CH)),
-        (F, dict(pmf=192, par=12, val=192, oh=768, junk=2 * CH, n4=4, sm=160, zall=144, rep=1024, turn=128, bd=128,
-                 gm=128, bits=24, seg=12, lv=192, lt=384, tabs=384, win=H, win2=H, rr=4 * CH, tf=192, t1=CH, t2=CH,
-                 z1=CH, z2=CH, zz=2 * CH, xm=CH, ys=H, uc=32, pp=192, bt=64))):
+        (I, dict(alt=128, cli=192, pmi=192, pa=192, pb=192, pj=192, tgi=4, gi=128)),
+        (U, dict(clu=192, offa=192, codea=192, offb=168, codeb=168)),
+        (B, dict(altb=128, alw=2048, arow=H, oneb=144, zin=144, iext=144, zb=144, zall=144, repb=1024, lw=CH, hl=384,
+                 win2=H, rr=7 * CH)),
+        (F, dict(pmf=192, par=12, val=192, oh=768, junk=2 * CH, n4=4, sm=160, rep=1024, turn=128, back=128, m2=8,
+                 yt=2 * CH, bd=128, gm=128, bits=24, seg=12, lv=192, lt=384, tabs=384, win=H, tf=192, t1=CH, t2=CH,
+                 t3=CH, z1=CH, z2=CH, zz=2 * CH, xm=3 * CH, ys=H, uc=32, pp=192, bt=64))):
     for _n, _c in _bufs.items():
         SCRATCH[_n] = ("sbuf", [128, _c], _d)
-for _n, _c, _d in (("sw", 48, B), ("dw", 48, B), ("sv", NL, F), ("dv", NL, F), ("dy", CH, F)):
+for _n, _c, _d in (("sw", 48, B), ("dw", 48, B), ("sv", NL, F), ("dv", NL, F), ("sr", 48, B), ("dr", 48, B), ("dy", CH, F)):
     SCRATCH[_n] = ("dram", [N, 128, _c], _d)
 for _k in range(8):
     SCRATCH["ps%d" % _k] = ("psum", [128, 512], F)
-SEMAPHORES = ["cv", "cs", "cp", "cg", "ls", "aw", "avs", "avd", "at", "ay", "az"] + ["d%d" % _k for _k in range(24)]
-WIDTH = {"lv": NL, "lt": 48, "ys": CH}
+SEMAPHORES = ["cv", "cs", "cp", "cg", "ls", "aw", "avs", "avd", "at", "ay", "az"] + ["b%d" % _k for _k in range(N)] \
+    + ["d%d" % _k for _k in range(24)]
+WIDTH = {"lv": NL, "lt": 48, "ys": CH, "yt": CH}
 
 
 def bits_of(engines):
@@ -35,6 +40,10 @@ def deal(engines, sizes):
     for s in sizes:
         out.append(bits_of(engines[k:k + s])); k += s
     return out
+
+
+def piece(d):
+    return ("yt", d - LATE) if d >= LATE else ("ys", d)
 
 
 def make_routes(cores, topo):
@@ -61,24 +70,28 @@ def make_routes(cores, topo):
         m = deal(off, [2, 2, 2])
         c["t"] = [[(a, n[k], ("lt", r), ("lt", r), "at") for k, a in enumerate((a0, a1))]
                   + [(cores[d], m[k], ("lt", r), ("lt", r), "at") for k, d in enumerate(same[r])]]
-        n = deal(on, [2, 2, 2, 2])
-        hand = [(via[d], n[k], ("sv", d), ("dv", d), "avd") for k, d in enumerate(by)]
         tiles = [(cores[d], m[k], ("sv", d), ("lv", r), "avs") for k, d in enumerate(same[r])]
-        rows = [(cores[d], m[k], ("sv", d), ("dv", r // 2), "avd") for k, d in enumerate(same[r])]
-        c["v"] = [hand + rows, tiles] if r % 2 == 0 else [hand + tiles]
+        if r in ROWS:
+            n = deal(on, [1] * 8)
+            c["v"] = [[(via[d], n[k], ("sv", d), ("dv", d), "avd") for k, d in enumerate(by)]
+                      + [(via[d], n[4 + k], ("sr", d), ("dr", d), "avd") for k, d in enumerate(by)]
+                      + [(cores[d], m[k], ("sr", d), ("dr", ROWS.index(r)), "avd") for k, d in enumerate(same[r])], tiles]
+        else:
+            n = deal(on, [2, 2, 2, 2])
+            c["v"] = [[(via[d], n[k], ("sv", d), ("dv", d), "avd") for k, d in enumerate(by)] + tiles]
         for d in same[r]:
-            c["y%d" % d] = [[(cores[d], bits_of(off), ("ys", d), ("dy", r), "ay")]]
+            c["y%d" % d] = [[(cores[d], bits_of(off), piece(d), ("dy", r), "b%d" % r)]]
         for k in range(2):
-            c["y%d" % by[k]] = [[(via[by[k]], bits_of(on), ("ys", by[k]), ("dy", by[k]), "ay")]]
+            c["y%d" % by[k]] = [[(via[by[k]], bits_of(on), piece(by[k]), ("dy", by[k]), "ay")]]
             d = by[2 + k]
-            c["y%d" % d] = [[(far[d], bits_of(off), ("ys", d), ("dy", r), ("ay", "az")[k])]]
+            c["y%d" % d] = [[(far[d], bits_of(off), piece(d), ("dy", r), ("ay", "az")[k])]]
             far_w[d].append(r); far_y[d].append((("ay", "az")[k], r))
         calls[me] = c
         for k, a in enumerate((a0, a1)):
             e = topo.engines(a, cores[by[0]]); mine = [by[k], by[2 + k]]
-            if r % 2 == 0:
+            if r in ROWS:
                 m = deal(e, [2, 2, 2, 2])
-                fv = [(cores[d], m[j], ("dv", d), ("dv", r // 2), "avd") for j, d in enumerate(mine)] \
+                fv = [(cores[d], m[j], ("dr", d), ("dr", ROWS.index(r)), "avd") for j, d in enumerate(mine)] \
                     + [(cores[d], m[2 + j], ("dv", d), ("lv", r), "avs") for j, d in enumerate(mine)]
             else:
                 m = deal(e, [4, 4])
@@ -87,11 +100,11 @@ def make_routes(cores, topo):
             steps[a] = [("aw", [(cores[by[k]], bits_of(e), ("dw", by[k]), ("dw", r), "aw")]),
                         ("avd", fv),
                         ("at", [(cores[d], m[j], ("lt", r), ("lt", r), "at") for j, d in enumerate(mine)]),
-                        ("ay", [(cores[by[k]], bits_of(e), ("dy", by[k]), ("dy", r), "ay")])]
+                        ("ay", [(cores[by[k]], bits_of(e), ("dy", by[k]), ("dy", r), "b%d" % r)])]
     for d in range(N):
         e = topo.engines(far[d], cores[d]); m = deal(e, [4, 4])
         steps[far[d]] = [("aw", [(cores[d], m[j], ("dw", r), ("dw", r), "aw") for j, r in enumerate(far_w[d])])] \
-            + [(s, [(cores[d], bits_of(e), ("dy", r), ("dy", r), "ay")]) for s, r in sorted(far_y[d])]
+            + [(s, [(cores[d], bits_of(e), ("dy", r), ("dy", r), "b%d" % r)]) for s, r in sorted(far_y[d])]
     every = [call for c in calls.values() for ph in c.values() for call in ph] + [call for s in steps.values() for _, call in s]
     for call in every:
         for dst, mask, _, _, sem in call:
@@ -267,9 +280,10 @@ def rank_program(g, core, T, topo):
     others = [r for r in range(N) if r != rank]
     landed("aw", "dw", others)
     landed("avs", "lv", others, NL)
-    landed("avd", "dv", [u for u in range(4) if 2 * u != rank])
+    landed("avd", "dr", [u for u, r in enumerate(ROWS) if r != rank])
     landed("at", "lt", others, 48)
-    landed("ay", "dy", others)
+    for r in others:
+        landed("b%d" % r, "dy", [r])
 
     dma("y", R("alt"), ext(T.al[:]), "al")
     dma("s", R("cli"), ext(T.cl[:]), "cl")
@@ -285,21 +299,23 @@ def rank_program(g, core, T, topo):
     mi = [R("par", 8 + s, 9 + s) for s in range(3)]
 
     memset(R("oneb"), 1.0)
-    memset(R("zin"), 1.0 / 32)
-    memset(R("win2", 0, 2048), 1.0)
+    memset(R("zin"), 1.0 / 16)
+    memset(R("win", 0, 1024), 1.0)
+    memset(R("win2"), 0.0)
     select(R("iext"), R("oneb"), [[-1, 144]], A.is_equal, 0, 1)
     iota(S("bits", 0, 8), [[0, 4], [1, 2]], 0, 0, True)
     iota(S("bits", 1, 8), [[0, 2], [1, 2], [0, 2]], 0, 0, True)
     iota(S("bits", 2, 8), [[1, 2], [0, 4]], 0, 0, True)
     select(R("zb"), R("zin"), [[-16, 9], [256, 16]], A.is_equal, -3840, 1)
     send("w", D("sw", 0, N))
-    select(R("rep"), R("win2", 0, 1024), [[-16, 8], [0, 8], [-1, 16]], A.is_equal, 0, 1)
-    select(R("bd"), R("win2", 0, 128), [[-16, 8], [0, 16]], A.is_ge, 0, 1)
+    select(R("rep"), R("win", 0, 1024), [[-16, 8], [0, 8], [-1, 16]], A.is_equal, 0, 1)
+    select(R("bd"), R("win", 0, 128), [[-16, 8], [0, 16]], A.is_ge, 0, 1)
     iota(R("seg"), [[0, 3], [1, 4]], 0, 0, True)
     iota(R("gi"), [[0, 8], [-1, 16]], 16, 1, False)
-    select(R("zall"), R("win2", 0, 144), [[-16, 9], [256, 16]], A.is_ge, -3840, 1)
+    select(R("zall"), R("oneb"), [[-16, 9], [256, 16]], A.is_ge, -3840, 1)
     select(R("bd"), R("bd"), [[16, 8], [0, 16]], A.is_ge, 15, -1)
-    select(R("turn"), R("win2", 0, 128), [[-1, 8], [-8, 16]], A.is_equal, 0, 1)
+    select(R("turn"), R("win", 0, 128), [[-1, 8], [-8, 16]], A.is_equal, 0, 1)
+    select(R("back"), R("win", 0, 128), [[-1, 16], [-16, 8]], A.is_equal, 0, 1)
     select(R("zall"), R("zall"), [[16, 9], [0, 16]], A.is_ge, 15, -1)
 
     copy(R("altb"), R("alt"))
@@ -321,39 +337,47 @@ def rank_program(g, core, T, topo):
     for k in range(16):
         mm(R("ps4", 0, 192), R("zb", 15 - k, 143 - k), R("arow", k, H, 16), k == 0, k == 15)
     act(R("repb"), R("rep"))
-    if rank % 2:
+    places = R("pmi")
+    if rank not in FIRST:
+        places = R("pj")
         ts(R("pa"), R("pmi"), 15, A.bitwise_and)
         ts(R("pb"), R("pmi"), 4, A.arith_shift_right)
     tt(E01, E[0], E[1], A.mult)
     tt(E12, E[1], E[2], A.mult)
+    if rank not in FIRST:
+        ts(R("tf"), R("pa"), 192.0, A.mult)
     ts(W1, E[0], st[0], A.mult)
     ts(K2, E[2], ju[2], A.mult)
-    if rank % 2:
-        ts(R("tf"), R("pa"), 192.0, A.mult)
+    if rank not in FIRST:
+        tt(R("pj"), R("tf"), R("pb"), A.add)
     ts(R("sm", 96, 100), R("sm", 0, 4), ju[0], A.mult)
     ts(R("sm", 104, 108), R("sm", 8, 12), ju[1], A.mult)
     tt(E012, E01, E[2], A.mult)
-    if rank % 2:
-        tt(R("pmf"), R("tf"), R("pb"), A.add)
-    else:
-        copy(R("pmf"), R("pmi"))
+    if rank in ROWS:
+        ts(R("pa"), places, 15, A.bitwise_and)
+        ts(R("pb"), places, 4080, A.bitwise_and)
     ts(W2, E01, st[0], A.mult, st[1], A.mult)
     ts(b1, E12, st[2], A.mult, ju[1], A.mult)
     ts(R("sm", 100, 104), R("sm", 24, 28), st[1], A.mult, ju[0], A.mult)
     ts(x0, E012, st[1], A.mult, st[2], A.mult)
+    if rank in ROWS:
+        copy(S("hl", 0, 192), R("pb"))
+        dma("y", (T.sr[:, 0:64, :], [("sr", 0, 1)]), S("hl", 0, 192), "sv")
     ts(R("seg"), R("seg"), 1.0, A.min)
     ts(AA, x0, st[0], A.mult)
     ts(b0, x0, ju[0], A.mult)
-    tt(R("val"), R("pmf"), R("ps4", 0, 192), A.add)
+    if rank in ROWS:
+        tt(S("hl", 1, 192), R("pa"), R("ps4", 0, 192), A.add)
+        dma("s", (T.sr[:, 64:128, :], [("sr", 1, 2)]), S("hl", 1, 192), "sv")
+    tt(R("val"), places, R("ps4", 0, 192), A.add)
     dma("y", D("sv", 0, N), R("val"), "sv")
-    own = (T.val[q0:q0 + 16, :], [("val", 0, 192)])
-    dma("y", S("lv", rank, NL), own, "olv")
-    if rank % 2 == 0:
-        dma("y", D("dv", rank // 2), own, "odv")
-    send("v", D("sv", 0, N))
+    dma("y", S("lv", rank, NL), (T.val[q0:q0 + 16, :], [("val", 0, 192)]), "olv")
+    send("v", D("sv", 0, N), D("sr", 0, 2))
+    if rank in ROWS:
+        dma("y", D("dr", ROWS.index(rank)), (T.sr[rank], [("sr", 0, 2)]), "odv")
 
-    ts(R("pa"), R("ps4", 0, 192), 32.0, A.mult)
-    ts(R("pb"), R("pa"), 3, A.bitwise_and)
+    ts(R("pj"), R("ps4", 0, 192), 16.0, A.mult)
+    ts(R("pb"), R("pj"), 3, A.bitwise_and)
     for k in range(4):
         ts(S("oh", k, 192), R("pb"), float(k), A.is_equal)
         act(S("oh", k, 192), S("oh", k, 192), acc=S("n4", k, 1))
@@ -373,7 +397,7 @@ def rank_program(g, core, T, topo):
     ts(x3, K1, m10, A.mult)
     tt(K0, x2, x3, A.add)
     send("t", S("lt", rank, 48))
-    memset(R("win2", 2048, H), 1.0)
+    tt(R("m2", 0, 5), R("gm", 0, 10, 2), R("gm", 1, 10, 2), A.add)
 
     def replicate(src, sel):
         for c in range(8):
@@ -388,82 +412,146 @@ def rank_program(g, core, T, topo):
         copy(R(off, lo, hi), R(bank, lo, hi))
         copy(R("tf", lo, hi), R(off, lo, hi))
         tt(R("pmf", lo, hi), R(bank, lo, hi), R("tf", lo, hi), A.subtract)
-        ts(R(code, lo, hi), R("pmf", lo, hi), 32.0, A.mult)
+        ts(R(code, lo, hi), R("pmf", lo, hi), 16.0, A.mult)
 
-    def compose(u):
-        src = ind(R("win2"), S("offa", 2 * u + 1, NL))
-        if u == 0:
-            ts(S("rr", u, CH), src, S("gm", u, 1), A.mult)
+    def oa(r):
+        return S("offa", r, NL)
+
+    def ob(k):
+        return S("offb", k, NL)
+
+    def ca(r):
+        return S("codea", r, NL)
+
+    def cb(k):
+        return S("codeb", k, NL)
+
+    def look(k, off, r, vector=False):
+        src, mask = ind(R("win2"), off), S("m2", ROWS.index(r), 1)
+        if vector:
+            ts(S("rr", k, CH), src, mask, A.mult)
         else:
-            act(S("rr", u, CH), src, scale=S("gm", u, 1))
+            act(S("rr", k, CH), src, scale=mask)
 
-    def fold(u0, u1):
+    def fold(k0, k1):
         for k in range(16):
-            mm(R("ps5", NL * u0, NL * u1), R("zall", 15 - k, 143 - k), R("rr", CH * u0 + k, CH * u1, 16), k == 0, k == 15)
+            mm(R("ps5", NL * k0, NL * k1), R("zall", 15 - k, 143 - k), R("rr", CH * k0 + k, CH * k1, 16), k == 0, k == 15)
+
+    def lists(k0, k1):
+        unpack("ps5", NL * k0, NL * k1, "offb", "codeb")
 
     for c in range(8):
-        dma("ys"[c % 2], (T.win2[16 * c:16 * c + 4, :], [("win2", 0, H)]), D("dv", 0, 4), "w2")
+        dma("ys"[c % 2], (T.win2[16 * c:16 * c + 10, :], [("win2", 0, H)]), D("dr", 0, 5), "w2")
     mm(R("ps4", 0, 192), R("turn"), R("lv"))
     unpack("ps4", 0, 192, "offa", "codea")
     mm(R("ps6", 0, 384), S("rep", rank, 128), R("lt"))
     act(R("tabs"), R("ps6", 0, 384))
-    compose(0)
-    fold(0, 1)
-    for u in range(1, 4):
-        compose(u)
 
     def tb(r, k):
         return S("tabs", 6 * r + k, 8)
 
-    def block(r, x, code, x2nd, code2nd, out):
+    def apply(r, code, x, out):
+        tt(S("zz", r % 2, CH), ind(tb(r, 2), code), x, A.mult)
+        tt(out, ind(S("bt", r, 8), code), S("zz", r % 2, CH), A.add)
+
+    def block(r, x, code, x2nd, code2nd, out, early=None, late=None):
         u = [S("uc", 4 * r + k, 1) for k in range(3)]
         p = [S("pp", 3 * r + k, 8) for k in range(3)]
         bank = R(("ps7", "ps4")[r % 2], 0, 8)
-        bt = S("bt", r, 8)
         tt(R("z1"), ind(tb(r, 0), code), x, A.mult)
         act(S("junk", 0, CH), x, acc=u[0])
         act(p[0], tb(r, 3), scale=u[0])
         mm(bank, R("gm"), p[0], True, False)
+        if early:
+            early()
         tt(R("z2"), ind(tb(r, 1), code), x, A.mult)
         act(S("junk", 1, CH), R("z1"), acc=u[1])
         act(p[1], tb(r, 4), scale=u[1])
         mm(bank, R("gm"), p[1], False, False)
-        if r == 0:
-            unpack("ps5", 0, NL, "offb", "codeb")
-            act(R("t2"), ind(R("win"), S("offb", 0, NL)))
-        ops.append(("v", lambda: g.vector.tensor_reduce(u[2][0], T.z2[:], AxisListType.X, A.add), reg(R("z2")), reg(u[2]), None))
-        ts(p[2], tb(r, 5), u[2], A.mult)
+        act(R("z2"), R("z2"), acc=u[2])
+        act(p[2], tb(r, 5), scale=u[2])
         mm(bank, R("gm"), p[2], False, True)
-        if r == 0:
-            fold(1, 4)
+        if late:
+            late()
         tt(S("zz", r % 2, CH), ind(tb(r, 2), code2nd), x2nd, A.mult)
-        copy(bt, bank)
-        tt(out, ind(bt, code2nd), S("zz", r % 2, CH), A.add)
+        copy(S("bt", r, 8), bank)
+        tt(out, ind(S("bt", r, 8), code2nd), S("zz", r % 2, CH), A.add)
+
+    def ys(r):
+        return S("ys", r, CH)
 
     def ship(r):
-        if r == rank:
-            dma("y", D("dy", rank), S("ys", r, CH), "oy")
+        out = ys(r)
+        if r >= LATE:
+            mm(R("ps%d" % (r % 2), 0, CH), R("back"), out)
+            out = S("yt", r - LATE, CH)
+            act(out, R("ps%d" % (r % 2), 0, CH))
+        if r != rank:
+            send("y%d" % r, out)
+        elif r >= LATE:
+            dma("y", ext(T.y[q0:q0 + 16, :]), out, "oy")
         else:
-            send("y%d" % r, S("ys", r, CH))
+            dma("y", D("dy", rank), out, "oy")
 
-    for u in range(4):
-        r = 2 * u
-        ca, cb = S("codea", r, NL), S("codea", r + 1, NL)
-        copy(R("t1"), ind(R("win"), S("offa", r, NL)))
-        if u:
-            act(R("t2"), ind(R("win"), S("offb", u, NL)))
-        block(r, R("t1"), ca, R("t2"), S("codeb", u, NL), R("xm"))
-        block(r + 1, R("xm"), cb, R("xm"), cb, S("ys", r + 1, CH))
-        ship(r + 1)
-        if u < 3:
-            replicate(S("ys", r + 1, CH), "rep")
-        tt(S("zz", 0, CH), ind(tb(r, 2), ca), R("t1"), A.mult)
-        tt(S("ys", r, CH), ind(S("bt", r, 8), ca), S("zz", 0, CH), A.add)
-        ship(r)
-        if u == 0:
-            unpack("ps5", NL, 4 * NL, "offb", "codeb")
+    t1, t2, t3, win = R("t1"), R("t2"), R("t3"), R("win")
+    xa, xb, xc = [S("xm", k, CH) for k in range(3)]
+    copy(t1, ind(win, oa(0)))
+    look(0, oa(1), 0, True)
+    look(1, oa(2), 1)
+    fold(0, 2)
+    look(3, oa(4), 3)
 
-    for c in range(8):
-        q = "s" if rank >= N - 2 and c % 2 else "y"
-        dma(q, ext(T.y[:, CH * c:CH * c + CH]), (T.dy[:, 16 * c:16 * c + 16, :], [("dy", 0, N)]), "out")
+    def late0():
+        lists(0, 2)
+        copy(t2, ind(win, ob(0)))
+        look(2, ob(1), 0)
+        look(4, oa(5), 4)
+        fold(2, 5)
+
+    def late1():
+        look(6, ob(4), 3)
+        look(5, oa(7), 6)
+        fold(5, 7)
+        apply(0, cb(2), t3, xc)
+
+    block(0, t1, ca(0), t2, cb(0), xa, None, late0)
+    lists(2, 5)
+    block(1, xa, ca(1), xc, cb(1), xb, lambda: act(t3, ind(win, ob(2))), late1)
+    block(2, xb, ca(2), xb, ca(2), ys(2))
+    ship(2)
+    replicate(ys(2), "rep")
+    apply(1, ca(1), xa, ys(1))
+    ship(1)
+    apply(0, ca(0), t1, ys(0))
+    ship(0)
+    lists(5, 7)
+
+    copy(t1, ind(win, oa(3)))
+    act(t3, ind(win, ob(6)))
+    block(3, t1, ca(3), t3, cb(6), xa, None, lambda: act(t2, ind(win, ob(3))))
+    block(4, xa, cb(4), xa, cb(4), xb)
+    block(5, xb, ca(5), xb, ca(5), ys(5))
+    ship(5)
+    replicate(ys(5), "rep")
+    apply(3, cb(3), t2, xc)
+    apply(4, ca(4), xc, ys(4))
+    ship(4)
+    apply(3, ca(3), t1, ys(3))
+    ship(3)
+
+    copy(t1, ind(win, oa(6)))
+    act(t2, ind(win, ob(5)))
+    block(6, t1, ca(6), t2, cb(5), xa)
+    block(7, xa, ca(7), xa, ca(7), ys(7))
+    ship(7)
+    apply(6, ca(6), t1, ys(6))
+    ship(6)
+
+    if rank >= LATE:
+        first = [r for r in others if topo.may_write(cores[r], core)]
+        for k, r in enumerate(first + [r for r in others if r not in first]):
+            dma("ys"[k % 2], ext(T.y[16 * r:16 * r + 16, :]), D("dy", r), "out")
+    else:
+        for c in range(8):
+            dma("y", ext(T.y[:, CH * c:CH * c + CH]), (T.dy[:, 16 * c:16 * c + 16, :], [("dy", 0, N)]), "out")
     emit(g, T, ops)

from concourse.bass import DstId, RemoteDMATransfer
from concourse.mybir import AluOpType, ActivationFunctionType

N, H, CH, NL = 8, 3072, 384, 24
SIM_CORES = 256
LATE = 6
FIRST = (0, 3, 6)
ROWS = (0, 1, 3, 4, 6)
F, B, I, U = "float32", "bfloat16", "int32", "uint16"

SCRATCH = {}
for _d, _bufs in (
        (I, dict(alt=128, cli=192, pmi=192, pa=192, pb=192, pj=192, tgi=4, gi=128)),
        (U, dict(clu=192, offa=192, codea=192, offb=168, codeb=168)),
        (B, dict(altb=128, alw=2048, arow=H, oneb=144, zin=144, iext=144, zb=144, zall=144, repb=1024, lw=CH, hl=384,
                 win2=H, rr=7 * CH)),
        (F, dict(pmf=192, par=12, val=192, oh=768, junk=2 * CH, n4=4, sm=160, rep=1024, turn=128, back=128, m2=8,
                 yt=2 * CH, bd=128, gm=128, bits=24, seg=12, lv=192, lt=384, tabs=384, win=H, tf=192, t1=CH, t2=CH,
                 t3=CH, z1=CH, z2=CH, zz=2 * CH, xm=3 * CH, ys=H, uc=32, pp=192, bt=64))):
    for _n, _c in _bufs.items():
        SCRATCH[_n] = ("sbuf", [128, _c], _d)
for _n, _c, _d in (("sw", 48, B), ("dw", 48, B), ("sv", NL, F), ("dv", NL, F), ("sr", 48, B), ("dr", 48, B), ("dy", CH, F)):
    SCRATCH[_n] = ("dram", [N, 128, _c], _d)
for _k in range(8):
    SCRATCH["ps%d" % _k] = ("psum", [128, 512], F)
SEMAPHORES = ["cv", "cs", "cp", "cg", "ls", "aw", "avs", "avd", "at", "ay", "az"] + ["b%d" % _k for _k in range(N)] \
    + ["d%d" % _k for _k in range(24)]
WIDTH = {"lv": NL, "lt": 48, "ys": CH, "yt": CH}


def bits_of(engines):
    m = 0
    for e in engines:
        m |= 1 << e
    return m


def deal(engines, sizes):
    out, k = [], 0
    for s in sizes:
        out.append(bits_of(engines[k:k + s])); k += s
    return out


def piece(d):
    return ("yt", d - LATE) if d >= LATE else ("ys", d)


def make_routes(cores, topo):
    cross = [[d for d in range(N) if d != r and not topo.may_write(cores[r], cores[d])] for r in range(N)]
    same = [[d for d in range(N) if d != r and topo.may_write(cores[r], cores[d])] for r in range(N)]
    near = [[c for c in topo.cores_of(cores[r]) if topo.die(c) != topo.die(cores[r]) and topo.may_write(c, cores[cross[r][0]])]
            for r in range(N)]
    far = [[c for c in range(SIM_CORES) if topo.mates(c, cores[d]) and topo.die(c) == topo.die(cores[d])
            and topo.may_write(c, cores[d])][0] for d in range(N)]
    calls, steps, arrive = {}, {}, {}
    far_w, far_y = [[] for _ in range(N)], [[] for _ in range(N)]
    for r in range(N):
        me = cores[r]
        off = topo.engines(me, cores[same[r][0]])
        on = [e for e in topo.engines(me, near[r][0]) if e not in off]
        by = sorted(cross[r], key=lambda d: (cross[r].index(d) - cross[d].index(r)) % len(cross[r]))
        a0, a1 = near[r][0], near[r][1]
        via = {by[0]: a0, by[1]: a1, by[2]: a0, by[3]: a1}
        c = {}
        m, n = deal(off, [2, 2, 2, 1, 1]), deal(on, [4, 4])
        c["w"] = [[(far[by[2 + k]], m[k], ("sw", by[2 + k]), ("dw", r), "aw") for k in range(2)]
                  + [(cores[d], m[2 + k], ("sw", d), ("dw", r), "aw") for k, d in enumerate(same[r])]
                  + [(via[by[k]], n[k], ("sw", by[k]), ("dw", by[k]), "aw") for k in range(2)]]
        m = deal(off, [2, 2, 2])
        c["t"] = [[(a, n[k], ("lt", r), ("lt", r), "at") for k, a in enumerate((a0, a1))]
                  + [(cores[d], m[k], ("lt", r), ("lt", r), "at") for k, d in enumerate(same[r])]]
        tiles = [(cores[d], m[k], ("sv", d), ("lv", r), "avs") for k, d in enumerate(same[r])]
        if r in ROWS:
            n = deal(on, [1] * 8)
            c["v"] = [[(via[d], n[k], ("sv", d), ("dv", d), "avd") for k, d in enumerate(by)]
                      + [(via[d], n[4 + k], ("sr", d), ("dr", d), "avd") for k, d in enumerate(by)]
                      + [(cores[d], m[k], ("sr", d), ("dr", ROWS.index(r)), "avd") for k, d in enumerate(same[r])], tiles]
        else:
            n = deal(on, [2, 2, 2, 2])
            c["v"] = [[(via[d], n[k], ("sv", d), ("dv", d), "avd") for k, d in enumerate(by)] + tiles]
        for d in same[r]:
            c["y%d" % d] = [[(cores[d], bits_of(off), piece(d), ("dy", r), "b%d" % r)]]
        for k in range(2):
            c["y%d" % by[k]] = [[(via[by[k]], bits_of(on), piece(by[k]), ("dy", by[k]), "ay")]]
            d = by[2 + k]
            c["y%d" % d] = [[(far[d], bits_of(off), piece(d), ("dy", r), ("ay", "az")[k])]]
            far_w[d].append(r); far_y[d].append((("ay", "az")[k], r))
        calls[me] = c
        for k, a in enumerate((a0, a1)):
            e = topo.engines(a, cores[by[0]]); mine = [by[k], by[2 + k]]
            if r in ROWS:
                m = deal(e, [2, 2, 2, 2])
                fv = [(cores[d], m[j], ("dr", d), ("dr", ROWS.index(r)), "avd") for j, d in enumerate(mine)] \
                    + [(cores[d], m[2 + j], ("dv", d), ("lv", r), "avs") for j, d in enumerate(mine)]
            else:
                m = deal(e, [4, 4])
                fv = [(cores[d], m[j], ("dv", d), ("lv", r), "avs") for j, d in enumerate(mine)]
            m = deal(e, [4, 4])
            steps[a] = [("aw", [(cores[by[k]], bits_of(e), ("dw", by[k]), ("dw", r), "aw")]),
                        ("avd", fv),
                        ("at", [(cores[d], m[j], ("lt", r), ("lt", r), "at") for j, d in enumerate(mine)]),
                        ("ay", [(cores[by[k]], bits_of(e), ("dy", by[k]), ("dy", r), "b%d" % r)])]
    for d in range(N):
        e = topo.engines(far[d], cores[d]); m = deal(e, [4, 4])
        steps[far[d]] = [("aw", [(cores[d], m[j], ("dw", r), ("dw", r), "aw") for j, r in enumerate(far_w[d])])] \
            + [(s, [(cores[d], bits_of(e), ("dy", r), ("dy", r), "b%d" % r)]) for s, r in sorted(far_y[d])]
    every = [call for c in calls.values() for ph in c.values() for call in ph] + [call for s in steps.values() for _, call in s]
    for call in every:
        for dst, mask, _, _, sem in call:
            arrive[(dst, sem)] = arrive.get((dst, sem), 0) + bin(mask).count("1")
    return calls, steps, arrive


def remote_call(g, core, T, topo, call):
    def side(key):
        name, k = key
        return T[name][:, WIDTH[name] * k:WIDTH[name] * (k + 1)] if name in WIDTH else T[name][k]
    if len(call) == 1:
        dst, mask, a, b, sem = call[0]
        rid, pid = topo.addr(dst, core)
        g.remote_dma(side(b), side(a), T.sem[sem], T.sem.ls, pid, rid, mask)
    else:
        tr = []
        for dst, mask, a, b, sem in call:
            rid, pid = topo.addr(dst, core)
            tr.append(RemoteDMATransfer(dst_ids=[DstId(rid=rid, pnc=pid)], dma_engine_mask=mask, remote_sem=T.sem[sem],
                                        src=side(a), dst=side(b)))
        g.remote_dma_fused(tr, local_sem=T.sem.ls)
    return sum(bin(t[1]).count("1") for t in call)


def emit(g, T, ops):
    queue = {"v": g.vector, "s": g.scalar, "p": g.tensor, "g": g, "y": g.sync}
    deps, needed = [], set()
    for n, (q, call, rd, wr, done) in enumerate(ops):
        mine = set()
        for k in range(n):
            q2, call2, rd2, wr2, done2 = ops[k]
            hit = False
            for (na, lo, hi) in rd:
                bank = na.startswith("ps") and q2 != q
                for (nb, l2, h2) in wr2 + (rd2 if bank else []):
                    if na == nb and (bank or (lo < h2 and l2 < hi)):
                        hit = True
            if not (q2 == q and ("+", 0, 0) in rd) and not (isinstance(done, str) and done == done2):
                for (na, lo, hi) in wr:
                    bank = na.startswith("ps") and q2 != q
                    for (nb, l2, h2) in wr2 + rd2:
                        if na == nb and (bank or (lo < h2 and l2 < hi)):
                            hit = True
            if hit and call is not None:
                mine.add(k)
        last = {}
        for k in mine:
            key = ops[k][0] if ops[k][4] is None else ("x", k)
            last[key] = max(last.get(key, -1), k)
        deps.append(sorted(last.values(), reverse=True)); needed.update(last.values())
    groups, total = {}, {}
    for q, call, rd, wr, done in ops:
        if isinstance(done, str) and done != "remote":
            groups.setdefault(done, "d%d" % len(groups))
            total[groups[done]] = total.get(groups[done], 0) + 16
        elif isinstance(done, tuple):
            total[done[0]] = done[1]
    mark, clock, known, count = {}, {}, {q: {} for q in queue}, {}
    for n, (q, call, rd, wr, done) in enumerate(ops):
        for k in deps[n]:
            sem, v = mark[k]
            if known[q].get(sem, 0) < v:
                queue[q].wait_ge(T.sem[sem], v)
                known[q][sem] = v
                for s2, v2 in clock[k].items():
                    known[q][s2] = max(known[q].get(s2, 0), v2)
        clock[n] = dict(known[q]) if call is not None else {}
        if call is None:
            mark[n] = done
        elif done == "remote":
            total["ls"] = total.get("ls", 0) + call()
        elif done is None:
            ins = call()
            if n in needed:
                sem = "c" + q
                count[sem] = count.get(sem, 0) + 1
                ins.then_inc(T.sem[sem], 1)
                mark[n] = (sem, count[sem]); total[sem] = count[sem]
        else:
            call().then_inc(T.sem[groups[done]], 16)
            mark[n] = (groups[done], total[groups[done]]); clock[n] = {}
    for sem, v in total.items():
        if all(known[q].get(sem, 0) < v for q in queue):
            g.wait_ge(T.sem[sem], v)


def rank_program(g, core, T, topo):
    cores = list(T.cores)
    calls, steps, arrive = make_routes(cores, topo)
    rank = T.rank_of(core)
    if rank is None:
        sent = 0
        for sem, call in steps.get(core, []):
            g.wait_ge(T.sem[sem], arrive[(core, sem)])
            sent += remote_call(g, core, T, topo, call)
        if sent:
            g.wait_ge(T.sem.ls, sent)
        return
    A, ACT = AluOpType, ActivationFunctionType
    ops = []

    def R(name, lo=0, hi=None, step=1):
        hi = SCRATCH[name][1][1] if hi is None else hi
        return (T[name][:, lo:hi:step] if step > 1 else T[name][:, lo:hi], [(name, lo, hi)])

    def S(name, k, n):
        return R(name, n * k, n * k + n)

    def ind(win, off):
        return (win[0].indirect(off[0]), win[1] + off[1])

    def reg(*xs):
        return [t for x in xs if isinstance(x, tuple) for t in x[1]]

    def ap(x):
        return x[0] if isinstance(x, tuple) else x

    def copy(o, i):
        ops.append(("v", lambda: g.vector.tensor_copy(o[0], i[0]), reg(i), reg(o), None))

    def tt(o, a, b, op):
        ops.append(("v", lambda: g.vector.tensor_tensor(o[0], a[0], b[0], op), reg(a, b), reg(o), None))

    def ts(o, a, s1, op0, s2=None, op1=None):
        if s2 is None:
            ops.append(("v", lambda: g.vector.tensor_scalar(o[0], a[0], ap(s1), None, op0), reg(a, s1), reg(o), None))
        else:
            ops.append(("v", lambda: g.vector.tensor_scalar(o[0], a[0], ap(s1), ap(s2), op0, op1), reg(a, s1, s2), reg(o), None))

    def memset(o, c):
        ops.append(("v", lambda: g.vector.memset(o[0], c), [], reg(o), None))

    def act(o, i, scale=None, acc=None):
        if acc is not None:
            ops.append(("s", lambda: g.scalar.activation(o[0], i[0], ACT.Copy, accum_out=acc[0]), reg(i), reg(o, acc), None))
        elif scale is not None:
            ops.append(("s", lambda: g.scalar.activation(o[0], i[0], ACT.Copy, scale=scale[0]), reg(i, scale), reg(o), None))
        else:
            ops.append(("s", lambda: g.scalar.activation(o[0], i[0], ACT.Copy), reg(i), reg(o), None))

    def mm(o, l, r, start=True, stop=True):
        ops.append(("p", lambda: g.tensor.matmul(o[0], l[0], r[0], start, stop),
                    reg(l, r) + ([] if start else [("+", 0, 0)]), reg(o), None))

    def select(o, i, pattern, op, base, cm):
        ops.append(("g", lambda: g.affine_select(o[0], i[0], pattern, op, 0.0, base, cm), reg(i), reg(o), None))

    def iota(o, pattern, base, cm, small):
        if small:
            ops.append(("g", lambda: g.iota(o[0], pattern, base, cm, allow_small_or_imprecise_dtypes=True), [], reg(o), None))
        else:
            ops.append(("g", lambda: g.iota(o[0], pattern, base, cm), [], reg(o), None))

    def dma(q, o, i, group):
        e = g.sync if q == "y" else g.scalar
        ops.append((q, lambda: e.dma_start(o[0], i[0]), reg(i), reg(o), group))

    def send(phase, *reads):
        for call in calls[core][phase]:
            ops.append(("g", lambda call=call: remote_call(g, core, T, topo, call), reg(*reads), [], "remote"))

    def landed(sem, name, slots, width=1):
        ops.append(("g", None, [], [(name, width * k, width * k + width) for k in slots], (sem, arrive[(core, sem)])))

    def D(name, lo, hi=None):
        return (T[name][lo], [(name, lo, lo + 1)]) if hi is None else (T[name][lo:hi], [(name, lo, hi)])

    def ext(x):
        return (x, [])

    q0 = 16 * rank
    others = [r for r in range(N) if r != rank]
    landed("aw", "dw", others)
    landed("avs", "lv", others, NL)
    landed("avd", "dr", [u for u, r in enumerate(ROWS) if r != rank])
    landed("at", "lt", others, 48)
    for r in others:
        landed("b%d" % r, "dy", [r])

    dma("y", R("alt"), ext(T.al[:]), "al")
    dma("s", R("cli"), ext(T.cl[:]), "cl")
    dma("y", D("sw", 0, N), ext(T.w[:]), "sw")
    dma("s", R("tgi", 0, 3), ext(T.tg[:]), "par")
    dma("s", R("par", 8, 11), ext(T.mi[:]), "par")
    dma("y", R("pmi"), ext(T.pm[:]), "pm")
    dma("s", R("par", 0, 3), ext(T.st[:]), "par")
    dma("s", R("par", 4, 7), ext(T.ju[:]), "par")
    dma("y", D("dw", rank), ext(T.w[q0:q0 + 16, :]), "ow")
    st = [R("par", s, s + 1) for s in range(3)]
    ju = [R("par", 4 + s, 5 + s) for s in range(3)]
    mi = [R("par", 8 + s, 9 + s) for s in range(3)]

    memset(R("oneb"), 1.0)
    memset(R("zin"), 1.0 / 16)
    memset(R("win", 0, 1024), 1.0)
    memset(R("win2"), 0.0)
    select(R("iext"), R("oneb"), [[-1, 144]], A.is_equal, 0, 1)
    iota(S("bits", 0, 8), [[0, 4], [1, 2]], 0, 0, True)
    iota(S("bits", 1, 8), [[0, 2], [1, 2], [0, 2]], 0, 0, True)
    iota(S("bits", 2, 8), [[1, 2], [0, 4]], 0, 0, True)
    select(R("zb"), R("zin"), [[-16, 9], [256, 16]], A.is_equal, -3840, 1)
    send("w", D("sw", 0, N))
    select(R("rep"), R("win", 0, 1024), [[-16, 8], [0, 8], [-1, 16]], A.is_equal, 0, 1)
    select(R("bd"), R("win", 0, 128), [[-16, 8], [0, 16]], A.is_ge, 0, 1)
    iota(R("seg"), [[0, 3], [1, 4]], 0, 0, True)
    iota(R("gi"), [[0, 8], [-1, 16]], 16, 1, False)
    select(R("zall"), R("oneb"), [[-16, 9], [256, 16]], A.is_ge, -3840, 1)
    select(R("bd"), R("bd"), [[16, 8], [0, 16]], A.is_ge, 15, -1)
    select(R("turn"), R("win", 0, 128), [[-1, 8], [-8, 16]], A.is_equal, 0, 1)
    select(R("back"), R("win", 0, 128), [[-1, 16], [-16, 8]], A.is_equal, 0, 1)
    select(R("zall"), R("zall"), [[16, 9], [0, 16]], A.is_ge, 15, -1)

    copy(R("altb"), R("alt"))
    for e in range(16):
        mm(S("ps%d" % (e // 4), e % 4, 128), R("iext", e, e + 128), R("altb"))
    copy(R("clu"), R("cli"))
    E = [S("sm", s, 8) for s in range(3)]
    E01, E12, E012, b0, b1, x0, x1 = [S("sm", 3 + k, 8) for k in range(7)]
    W1, W2, AA, K0, K1, K2 = [S("lt", 6 * rank + k, 8) for k in range(6)]
    copy(R("sm", 80, 83), R("tgi", 0, 3))
    for s in range(3):
        ts(E[s], S("bits", s, 8), R("sm", 80 + s, 81 + s), A.is_equal, mi[s], A.max)
    copy(S("alw", 0, 512), R("ps0"))
    act(S("alw", 2, 512), R("ps2"))
    copy(S("alw", 1, 512), R("ps1"))
    act(S("alw", 3, 512), R("ps3"))
    copy(R("arow", 0, 1536), ind(R("alw"), R("clu", 0, 96)))
    act(R("arow", 1536, H), ind(R("alw"), R("clu", 96, 192)))
    for k in range(16):
        mm(R("ps4", 0, 192), R("zb", 15 - k, 143 - k), R("arow", k, H, 16), k == 0, k == 15)
    act(R("repb"), R("rep"))
    places = R("pmi")
    if rank not in FIRST:
        places = R("pj")
        ts(R("pa"), R("pmi"), 15, A.bitwise_and)
        ts(R("pb"), R("pmi"), 4, A.arith_shift_right)
    tt(E01, E[0], E[1], A.mult)
    tt(E12, E[1], E[2], A.mult)
    if rank not in FIRST:
        ts(R("tf"), R("pa"), 192.0, A.mult)
    ts(W1, E[0], st[0], A.mult)
    ts(K2, E[2], ju[2], A.mult)
    if rank not in FIRST:
        tt(R("pj"), R("tf"), R("pb"), A.add)
    ts(R("sm", 96, 100), R("sm", 0, 4), ju[0], A.mult)
    ts(R("sm", 104, 108), R("sm", 8, 12), ju[1], A.mult)
    tt(E012, E01, E[2], A.mult)
    if rank in ROWS:
        ts(R("pa"), places, 15, A.bitwise_and)
        ts(R("pb"), places, 4080, A.bitwise_and)
    ts(W2, E01, st[0], A.mult, st[1], A.mult)
    ts(b1, E12, st[2], A.mult, ju[1], A.mult)
    ts(R("sm", 100, 104), R("sm", 24, 28), st[1], A.mult, ju[0], A.mult)
    ts(x0, E012, st[1], A.mult, st[2], A.mult)
    if rank in ROWS:
        copy(S("hl", 0, 192), R("pb"))
        dma("y", (T.sr[:, 0:64, :], [("sr", 0, 1)]), S("hl", 0, 192), "sv")
    ts(R("seg"), R("seg"), 1.0, A.min)
    ts(AA, x0, st[0], A.mult)
    ts(b0, x0, ju[0], A.mult)
    if rank in ROWS:
        tt(S("hl", 1, 192), R("pa"), R("ps4", 0, 192), A.add)
        dma("s", (T.sr[:, 64:128, :], [("sr", 1, 2)]), S("hl", 1, 192), "sv")
    tt(R("val"), places, R("ps4", 0, 192), A.add)
    dma("y", D("sv", 0, N), R("val"), "sv")
    dma("y", S("lv", rank, NL), (T.val[q0:q0 + 16, :], [("val", 0, 192)]), "olv")
    send("v", D("sv", 0, N), D("sr", 0, 2))
    if rank in ROWS:
        dma("y", D("dr", ROWS.index(rank)), (T.sr[rank], [("sr", 0, 2)]), "odv")

    ts(R("pj"), R("ps4", 0, 192), 16.0, A.mult)
    ts(R("pb"), R("pj"), 3, A.bitwise_and)
    for k in range(4):
        ts(S("oh", k, 192), R("pb"), float(k), A.is_equal)
        act(S("oh", k, 192), S("oh", k, 192), acc=S("n4", k, 1))
    ts(R("gi"), R("gi"), 15, A.bitwise_and)
    for k in range(3):
        mm(S("ps5", k, 4), R("bd"), R("n4"))
    ts(R("gm"), R("gi"), 0.0, A.is_equal)
    tt(R("sm", 112, 124), R("sm", 96, 108), R("ps5", 0, 12), A.mult)
    ops.append(("v", lambda: g.vector.tensor_tensor_scan(T.sm[:, 128:140], T.seg[:], T.sm[:, 112:124], 0.0, A.mult, A.add),
                reg(R("seg"), R("sm", 112, 124)), reg(R("sm", 128, 140)), None))
    m10, m20, m21 = R("sm", 131, 132), R("sm", 135, 136), R("sm", 139, 140)
    x2, x3 = R("sm", 144, 152), R("sm", 152, 160)
    ts(x0, K2, m21, A.mult)
    ts(x1, K2, m20, A.mult)
    tt(K1, x0, b1, A.add)
    tt(x2, x1, b0, A.add)
    ts(x3, K1, m10, A.mult)
    tt(K0, x2, x3, A.add)
    send("t", S("lt", rank, 48))
    tt(R("m2", 0, 5), R("gm", 0, 10, 2), R("gm", 1, 10, 2), A.add)

    def replicate(src, sel):
        for c in range(8):
            bank = R("ps%d" % (c % 4), 0, CH)
            mm(bank, S(sel, c, 128), src)
            act(S("win", c, CH), bank)

    dma("s", R("lw"), D("dw", 0, N), "lw")
    replicate(R("lw"), "repb")

    def unpack(bank, lo, hi, off, code):
        copy(R(off, lo, hi), R(bank, lo, hi))
        copy(R("tf", lo, hi), R(off, lo, hi))
        tt(R("pmf", lo, hi), R(bank, lo, hi), R("tf", lo, hi), A.subtract)
        ts(R(code, lo, hi), R("pmf", lo, hi), 16.0, A.mult)

    def oa(r):
        return S("offa", r, NL)

    def ob(k):
        return S("offb", k, NL)

    def ca(r):
        return S("codea", r, NL)

    def cb(k):
        return S("codeb", k, NL)

    def look(k, off, r, vector=False):
        src, mask = ind(R("win2"), off), S("m2", ROWS.index(r), 1)
        if vector:
            ts(S("rr", k, CH), src, mask, A.mult)
        else:
            act(S("rr", k, CH), src, scale=mask)

    def fold(k0, k1):
        for k in range(16):
            mm(R("ps5", NL * k0, NL * k1), R("zall", 15 - k, 143 - k), R("rr", CH * k0 + k, CH * k1, 16), k == 0, k == 15)

    def lists(k0, k1):
        unpack("ps5", NL * k0, NL * k1, "offb", "codeb")

    for c in range(8):
        dma("ys"[c % 2], (T.win2[16 * c:16 * c + 10, :], [("win2", 0, H)]), D("dr", 0, 5), "w2")
    mm(R("ps4", 0, 192), R("turn"), R("lv"))
    unpack("ps4", 0, 192, "offa", "codea")
    mm(R("ps6", 0, 384), S("rep", rank, 128), R("lt"))
    act(R("tabs"), R("ps6", 0, 384))

    def tb(r, k):
        return S("tabs", 6 * r + k, 8)

    def apply(r, code, x, out):
        tt(S("zz", r % 2, CH), ind(tb(r, 2), code), x, A.mult)
        tt(out, ind(S("bt", r, 8), code), S("zz", r % 2, CH), A.add)

    def block(r, x, code, x2nd, code2nd, out, early=None, late=None):
        u = [S("uc", 4 * r + k, 1) for k in range(3)]
        p = [S("pp", 3 * r + k, 8) for k in range(3)]
        bank = R(("ps7", "ps4")[r % 2], 0, 8)
        tt(R("z1"), ind(tb(r, 0), code), x, A.mult)
        act(S("junk", 0, CH), x, acc=u[0])
        act(p[0], tb(r, 3), scale=u[0])
        mm(bank, R("gm"), p[0], True, False)
        if early:
            early()
        tt(R("z2"), ind(tb(r, 1), code), x, A.mult)
        act(S("junk", 1, CH), R("z1"), acc=u[1])
        act(p[1], tb(r, 4), scale=u[1])
        mm(bank, R("gm"), p[1], False, False)
        act(R("z2"), R("z2"), acc=u[2])
        act(p[2], tb(r, 5), scale=u[2])
        mm(bank, R("gm"), p[2], False, True)
        if late:
            late()
        tt(S("zz", r % 2, CH), ind(tb(r, 2), code2nd), x2nd, A.mult)
        copy(S("bt", r, 8), bank)
        tt(out, ind(S("bt", r, 8), code2nd), S("zz", r % 2, CH), A.add)

    def ys(r):
        return S("ys", r, CH)

    def ship(r):
        out = ys(r)
        if r >= LATE:
            mm(R("ps%d" % (r % 2), 0, CH), R("back"), out)
            out = S("yt", r - LATE, CH)
            act(out, R("ps%d" % (r % 2), 0, CH))
        if r != rank:
            send("y%d" % r, out)
        elif r >= LATE:
            dma("y", ext(T.y[q0:q0 + 16, :]), out, "oy")
        else:
            dma("y", D("dy", rank), out, "oy")

    t1, t2, t3, win = R("t1"), R("t2"), R("t3"), R("win")
    xa, xb, xc = [S("xm", k, CH) for k in range(3)]
    copy(t1, ind(win, oa(0)))
    look(0, oa(1), 0, True)
    look(1, oa(2), 1)
    fold(0, 2)
    look(3, oa(4), 3)

    def late0():
        lists(0, 2)
        copy(t2, ind(win, ob(0)))
        look(2, ob(1), 0)
        look(4, oa(5), 4)
        fold(2, 5)

    def late1():
        look(6, ob(4), 3)
        look(5, oa(7), 6)
        fold(5, 7)
        apply(0, cb(2), t3, xc)

    block(0, t1, ca(0), t2, cb(0), xa, None, late0)
    lists(2, 5)
    block(1, xa, ca(1), xc, cb(1), xb, lambda: act(t3, ind(win, ob(2))), late1)
    block(2, xb, ca(2), xb, ca(2), ys(2))
    ship(2)
    replicate(ys(2), "rep")
    apply(1, ca(1), xa, ys(1))
    ship(1)
    apply(0, ca(0), t1, ys(0))
    ship(0)
    lists(5, 7)

    copy(t1, ind(win, oa(3)))
    act(t3, ind(win, ob(6)))
    block(3, t1, ca(3), t3, cb(6), xa, None, lambda: act(t2, ind(win, ob(3))))
    block(4, xa, cb(4), xa, cb(4), xb)
    block(5, xb, ca(5), xb, ca(5), ys(5))
    ship(5)
    replicate(ys(5), "rep")
    apply(3, cb(3), t2, xc)
    apply(4, ca(4), xc, ys(4))
    ship(4)
    apply(3, ca(3), t1, ys(3))
    ship(3)

    copy(t1, ind(win, oa(6)))
    act(t2, ind(win, ob(5)))
    block(6, t1, ca(6), t2, cb(5), xa)
    block(7, xa, ca(7), xa, ca(7), ys(7))
    ship(7)
    apply(6, ca(6), t1, ys(6))
    ship(6)

    if rank >= LATE:
        first = [r for r in others if topo.may_write(cores[r], core)]
        for k, r in enumerate(first + [r for r in others if r not in first]):
            dma("ys"[k % 2], ext(T.y[16 * r:16 * r + 16, :]), D("dy", r), "out")
    else:
        for c in range(8):
            dma("y", ext(T.y[:, CH * c:CH * c + CH]), (T.dy[:, 16 * c:16 * c + 16, :], [("dy", 0, N)]), "out")
    emit(g, T, ops)
